import numpy as np, ml_dtypes
CORES = [66,74,82,90,194,202,210,218]
N = 8
BF = ml_dtypes.bfloat16
V, A, S, RO = 2048, 256, 1, 3
def parts(rng):
    od = np.argsort(np.arange(V) + rng.choice(np.array([24, 400, 4 * V]), (N, 8, 1)) * rng.random((N, 8, V)), axis=-1); inv = np.argsort(od, axis=-1)
    c = rng.choice(np.array([8, 16]), (1, 8, 1, 1)); e = rng.choice(np.array([1.0, 1.5, 2.0]), (1, 8, 1, 1))
    w = np.arange(V) // c * c + (c * rng.random((N, 8, 16, V)) ** e).astype(np.int64)
    w = np.where(rng.random(w.shape) < 0.125, rng.integers(0, V, w.shape), w)
    nb = np.take_along_axis(np.take_along_axis(od[:, :, None], w, 3), inv[:, :, None], 3)
    x = np.minimum(np.maximum(rng.integers(0, 16, (1, 1, 16, V)) + rng.integers(-2, 3, (N, 8, 16, V)), 0), 15)
    return od, nb, np.take_along_axis(x, inv[:, :, None], 3)
def seeds(rng, od, m, lo, hi):
    mp = np.full((N, 8, V), V); iv = np.full((N, 8, V), V); ky = np.full((N, 8, V), 1000)
    for r in range(N):
        q = (r + 1) % N
        for g in range(8):
            h = (g + (r == N - 1)) % 8
            p = np.flatnonzero(m[r, g][od[r, g]]); w = p + 0
            e = np.flatnonzero(rng.random(len(p)) < 0.1); w[e] = p[rng.permutation(e)]
            u = od[r, g][p]; v = od[q, h][w]
            mp[r, g, u] = v; iv[q, h, v] = u; ky[q, h, v] = rng.integers(lo, hi, len(v))
    return mp, iv, ky
def pack(x, nb, mp, iv, ky):
    return {"x": np.ascontiguousarray(x.reshape(N, 128, V)).astype(np.float32).astype(BF), "nb": np.ascontiguousarray(nb.reshape(N, 128, V)).astype(np.int32),
            "mp": mp.astype(np.int32), "iv": iv.astype(np.int32), "ky": ky.astype(np.int32)}
def setup_inputs(rng):
    od, nb, x = parts(rng); m = rng.random((N, 8, V)) < rng.choice(np.array([0.35, 0.5, 0.65]), (N, 8, 1))
    return pack(x, nb, *seeds(rng, od, m, -80, 160))
def setup_inputs_room(rng):
    od, nb, x = parts(rng); m = np.ones((N, 8, V), bool); T = V // S
    for r in range(N):
        for k in range(S):
            c = np.array([A, A + 1, T, A - 1, 1, 0, A, A + 1])
            if r or k: c = rng.permutation(c)
            for g in range(8): m[r, g, k * T + rng.permutation(T)[:int(c[g])]] = False
    return pack(x, nb, *seeds(rng, od, m, -80, 300))
def setup_inputs_ties(rng):
    od, nb, x = parts(rng); m = rng.random((N, 8, V)) < 0.5
    x[:, :4] = x[:1, :1, :, :1] + 0
    x[:, 4:] = np.where(x[:, 4:, :1] < 8, 3, 4)
    mp, iv, ky = seeds(rng, od, m, 0, 1)
    ky = np.where(iv < V, rng.choice(np.array([-64, -48, -47, -33, -32, -31, -17, 999]), (N, 8, V)), 1000)
    return pack(x, nb, mp, iv, ky)
def setup_inputs_alike(rng):
    od, nb, x = parts(rng); m = rng.random((N, 8, V)) < 0.5; T = V // S
    nb[:, 0] = nb[:, 0, :1] + 0; x[:, 0] = x[:1, 0, :, :1] + 0
    m[:, 1, 0] = True; m[:, 1, V - 1] = True; nb[:, 1] = rng.choice(np.array([0, V - 1]), (N, 16, V))
    m[:, 2, 0] = False
    for r in range(N): nb[r, 2] = rng.choice(np.flatnonzero(~m[r, 2]), (16, V))
    nb[:, 3, :8] = np.arange(V)
    nb[:, 4, 1::2] = nb[:, 4, 0::2] + 0
    nb[:, 5, 8:] = nb[:, 5, :8] + 0
    few = np.array([0, 1, V // 2, V - 1]); m[:, 6, few] = True; nb[:, 6] = rng.choice(few, (N, 16, V))
    o = np.arange(V) % T; m[:, 7] = (o >= 3) & (o < T - 40)
    mp, iv, ky = seeds(rng, od, m, -80, 300)
    ky[:, 0] = np.where((iv[:, 0] < V) & (rng.random((N, V)) < 0.3), -256, ky[:, 0])
    return pack(x, nb, mp, iv, ky)
def setup_inputs_evict(rng):
    od, nb, x = parts(rng); m = rng.random((N, 8, V)) < rng.choice(np.array([0.8, 0.85, 0.9]), (N, 8, 1))
    return pack(x, nb, *seeds(rng, od, m, 209, 1000))
def setup_inputs_spread(rng):
    od, nb, x = parts(rng); m = rng.random((N, 8, V)) < rng.choice(np.array([0.05, 0.2, 0.5, 0.8, 0.95]), (N, 8, 1))
    y = (16 * rng.random((N, 8, 16, V)) ** np.exp2(rng.integers(-2, 4, (N, 8, 1, V)))).astype(np.int64)
    x = np.where(rng.random((N, 8, 1, V)) < 0.5, np.minimum(y, 15), x)
    low = (V * rng.random(nb.shape) ** 6).astype(np.int64)
    nb = np.where(rng.random(nb.shape) < rng.choice(np.array([0.02, 0.2]), (N, 8, 1, 1)), np.minimum(low, V - 1), nb)
    return pack(x, nb, *seeds(rng, od, m, -256, 1000))
def check_inputs(d):
    bad = []; x = np.asarray(d["x"]).astype(np.float32)
    if not np.all((x >= 0) & (x <= 15) & (x == np.floor(x))): bad.append("numbers of x")
    for k, lo, hi in (("nb", 0, V - 1), ("mp", 0, V), ("iv", 0, V), ("ky", -256, 1000)):
        if np.min(d[k]) < lo or np.max(d[k]) > hi: bad.append("range of " + k)
    if bad: return bad
    mp = np.asarray(d["mp"]).astype(np.int64); iv = np.asarray(d["iv"]).astype(np.int64); ky = np.asarray(d["ky"])
    r, g, u = np.nonzero(mp < V)
    if np.any(iv[(r + 1) % N, np.where(r == N - 1, g + 1, g) % 8, mp[r, g, u]] != u): bad.append("iv is not the inverse of mp")
    r, g, v = np.nonzero(iv < V)
    if np.any(mp[(r - 1) % N, np.where(r == 0, g + 7, g) % 8, iv[r, g, v]] != v): bad.append("mp is not the inverse of iv")
    if np.any((ky == 1000) != (iv == V)): bad.append("keys of unmatched nodes")
    return bad
def reference(x, nb, mp, iv, ky):
    X = x.astype(np.float32).astype(np.int64).reshape(N, 8, 16, V); B = nb.astype(np.int64).reshape(N, 8, 16, V)
    M = mp.astype(np.int64); I = iv.astype(np.int64); K = ky.astype(np.int64); T = V // S
    for t in range(RO):
        lo = (t % S) * T; todo = []
        row = ((np.arange(16) + t) & 15)[:, None]
        for r in range(N):
            q = (r + 1) % N
            for g in range(8):
                h = (g + 1) % 8 if r == N - 1 else g
                u = lo + np.flatnonzero(M[r, g, lo:lo + T] == V)[:A]
                z = M[r, g][B[r, g][:, u]]; has = z < V
                v = np.where(has, B[q, h][row, np.minimum(z, V - 1)], 0)
                s = np.add.reduce(((v[:, None] == v[None]) & has[None]).astype(np.int64), axis=1)
                d = np.add.reduce(np.abs(X[r, g][:, u][:, None] - X[q, h][:, v]), axis=0)
                sc = np.where(has & (s >= 2), d - 16 * s, 5000)
                j = np.argmin(sc, axis=0); a = np.arange(len(u)); best = sc[j, a]; v = v[j, a]
                a = np.flatnonzero(best < 5000); u, v, best = u[a], v[a], best[a]
                o = np.lexsort((u, best, v)); u, v, best = u[o], v[o], best[o]
                first = np.ones(len(v), bool); first[1:] = v[1:] != v[:-1]
                a = np.flatnonzero(first & (best < K[q, h][v])); u, v, best = u[a], v[a], best[a]
                todo.append((r, g, q, h, u, v, best, (3 * X[q, h][:, v] + X[r, g][:, u]) >> 2))
        for r, g, q, h, u, v, best, col in todo:
            old = I[q, h][v]; M[r, g, old[old < V]] = V
            M[r, g, u] = v; I[q, h, v] = u; K[q, h, v] = best; X[q, h][:, v] = col
    return {"ym": M.astype(np.float32), "yk": K.astype(np.float32)}

import numpy as np
from concourse.mybir import AluOpType as A, ActivationFunctionType as AF, AxisListType as AX

V = 2048
BIG = 131072.0
f32, bf, f16, i32, u16 = "float32", "bfloat16", "float16", "int32", "uint16"
SB = {}
for _d, _txt in [
    (i32, "BH:2080 BG:2080 BS:2048 NI:2,64 KN:2,128 DI:4,128 DI2:4,128 CI:16 QI:16,5 TA:16 TB:16 TI:17 TJ:17 TG:4"),
    (f32, "F:2080 NF:4,2,16 MW:128 CT:136 NO:128 CQ:16,5 SQ:16,4 SL:16,4 T3:16 DU:48 O1:16 U2:16 U4:16 UF:16 MO:128 LM:128 KO:128 "
          "CF:16 TC:16 E16:16"),
    (u16, "sML:128 ML:128 sWL:272 WL:272 BL:16 VL:256 VW:16 SU:16 TL:16 TV:16 LT0:16 LT1:16 RT:16 UN:16"),
    (f16, "R16:4096 UB:256 VH:256 KS:256 XB:32 PN:16 RB:128 RF:128 UH:16 WH:512 WK:144 WI:144 IH:128 DS:16,128 DM:8,128"),
    (bf, "XH:2304 XG:2304 XS:2048 Mt:2816 KI:2304 E:4096 XR:4096 LO:2,8,128 sDG:4,2,64 DG:4,2,64 DK:4,128 sXU:512 XU:512 FL:128 "
         "RS:128 CB:8 C1:16,8,16 BB:16 C2:256 AD:2048 EQ:2048 S1:256 S2:256 QR:16,16 QL:16,16 MV:512 ZE:256 ZO:256 H4:4 T1:256 "
         "T2:256 XN:256 LX0:256 LX1:256 RX:256 IA:256 JC:17 GM:128 BO:128 NB:128 NU:128 G8:8 G8S:8 W1:144 WM:144 WB:144 ID:128 "
         "I16:128 IS:128 IP:128 PM:128 I3:128 ZM:7,128 ON:2"),
]:
    for _w in _txt.split():
        SB[_w.split(":")[0]] = ([int(_x) for _x in _w.split(":")[1].split(",")], _d)
SCRATCH = {k: ("sbuf", [128] + s, d) for k, (s, d) in SB.items()}
SCRATCH["PS"] = ("psum", [128, 4096], f32)
ARR = ["ml", "wl", "xu", "dg", "xg", "bg", "lx0", "lx1", "lt0", "lt1", "lm"]
SEMAPHORES = ["cv", "cs", "cp", "cg"] + ["a_" + a for a in ARR] + ["s_" + a for a in ARR] + ["d%d" % i for i in range(48)]
COMPUTE = {"v": "cv", "s": "cs", "p": "cp", "g": "cg"}
ALL = slice(None)
S_ = slice


def rank_program(g, core, T, topo):
    rank = T.rank_of(core)
    if rank is None:
        return
    n = len(T.cores)
    nxt, prv = T.cores[(rank + 1) % n], T.cores[(rank - 1) % n]
    turn_out, turn_in = rank == n - 1, rank == 0
    Q = {"v": g.vector, "s": g.scalar, "p": g.tensor, "g": g, "y": g.sync}
    ops = []
    flat = {k: np.arange(int(np.prod(s))).reshape(s) for k, (s, d) in SB.items()}
    lastw = {k: np.full(v.size, -1) for k, v in flat.items()}
    lastr = {k: {} for k in flat}
    bank = [dict() for _ in range(8)]
    nd = [0]
    fams = {}

    def B(name, *idx, p=ALL):
        ap = T[name][(p,) + idx] if idx else T[name][p]
        if name == "PS":
            return (ap, [("PS", np.unique(np.arange(4096)[idx] // 512))], [])
        return (ap, [(name, flat[name][idx].ravel())], [])

    def R(name, lo, hi, step=1):
        return B(name, S_(lo, hi, step))

    def PS(b, lo, hi, step=1):
        return R("PS", 512 * b + lo, 512 * b + hi, step)

    def IND(win, off):
        return (win[0].indirect(off[0]), win[1], off[1])

    def add(q, fn, reads, writes, sem=None, lane=None, fam=None):
        me = len(ops)
        lane = lane or q
        deps = set()
        rd, wr = [], []
        for r in reads:
            if isinstance(r, tuple):
                rd += r[1] + r[2]
        for w in writes:
            wr += w[1]
            rd += w[2]
        for name, el in rd + wr:
            if name == "PS":
                for b in el:
                    deps.update(o for k, o in bank[int(b)].items() if k != lane)
                    bank[int(b)] = {lane: me}
        rd = [x for x in rd if x[0] != "PS"]
        wr = [x for x in wr if x[0] != "PS"]
        for name, el in rd:
            deps.update(int(x) for x in np.unique(lastw[name][el]) if x >= 0)
        for name, el in wr:
            deps.update(int(x) for x in np.unique(lastw[name][el]) if x >= 0 and ops[int(x)]["lane"] != lane)
            for k, arr in lastr[name].items():
                if k != lane:
                    deps.update(int(x) for x in np.unique(arr[el]) if x >= 0)
        for name, el in rd:
            lastr[name].setdefault(lane, np.full(lastw[name].size, -1))[el] = me
        for name, el in wr:
            lastw[name][el] = me
        deps.discard(me)
        if fam:
            mates = [d for d in deps if ops[d]["fam"] == fam]
            deps.difference_update(fams.get(fam, []))
            for d in mates:
                deps.update(ops[d]["deps"])
        for d in list(deps):
            if ops[d]["fam"]:
                deps.update(fams[ops[d]["fam"]])
        if fam:
            fams.setdefault(fam, []).append(me)
        ops.append({"q": q, "fn": fn, "deps": deps, "sem": sem, "lane": lane, "fam": fam})

    def ap(x):
        return x[0] if isinstance(x, tuple) else x

    def copy(o, i):
        add("v", lambda: g.vector.tensor_copy(o[0], i[0]), [i], [o])

    def tt(o, a, b, op):
        add("v", lambda: g.vector.tensor_tensor(o[0], a[0], b[0], op), [a, b], [o])

    def ts(o, a, s1, op0, s2=None, op1=None):
        if op1 is None:
            add("v", lambda: g.vector.tensor_scalar(o[0], a[0], ap(s1), None, op0), [a, s1], [o])
        else:
            add("v", lambda: g.vector.tensor_scalar(o[0], a[0], ap(s1), ap(s2), op0, op1), [a, s1, s2], [o])

    def mset(o, c):
        add("v", lambda: g.vector.memset(o[0], c), [], [o])

    def act(o, i, func, bias=None, scale=None):
        kw = {}
        if bias is not None:
            kw["bias"] = ap(bias)
        if scale is not None:
            kw["scale"] = ap(scale)
        add("s", lambda: g.scalar.activation(o[0], i[0], func, **kw), [i, bias, scale], [o])

    def lin(o, i, a, b=None):
        act(o, i, AF.Identity, scale=a, bias=b)

    def mm(o, l, r, start=True, stop=True):
        add("p", lambda: g.tensor.matmul(o[0], l[0], r[0], start, stop), [l, r], [o])

    def iota(o, pat, base, cm, flag=True):
        if flag:
            add("g", lambda: g.iota(o[0], pat, base, cm, allow_small_or_imprecise_dtypes=True), [], [o])
        else:
            add("g", lambda: g.iota(o[0], pat, base, cm), [], [o])

    def asel(o, i, pat, cmp, fill, base, cm):
        add("g", lambda: g.affine_select(o[0], i[0], pat, cmp, fill, base, cm), [i], [o])

    def dma(q, o, i, fam=None):
        s = "d%d" % nd[0]
        nd[0] += 1
        add(q, lambda: Q[q].dma_start(ap(o), ap(i)), [i], [o] if isinstance(o, tuple) else [], sem=(s, 16), lane=s, fam=fam)

    def send(name, dst, o, i):
        rid, pid = topo.addr(dst, core)
        m = topo.mask(core, dst)
        add("g", lambda: g.remote_dma(T[o[0]][:, o[1]:o[2]], i[0], T.sem["a_" + name], T.sem["s_" + name], pid, rid, m),
            [i], [], sem=("s_" + name, len(topo.engines(core, dst))), lane="s_" + name)

    def arrive(name, src, o):
        add(None, None, [], [o], sem=("a_" + name, len(topo.engines(src, core))), lane="a_" + name)

    col = lambda name, c: R(name, c, c + 1)
    AND, SHR = A.bitwise_and, A.arith_shift_right

    def turn(dst, src, fam):
        dma("y", B(dst, p=S_(16, 128)), src(0, 112), fam)
        dma("y", B(dst, p=S_(0, 16)), src(112, 128), fam)

    arrive("ml", prv, B("ML")); arrive("wl", prv, B("WL")); arrive("xu", prv, B("XU")); arrive("dg", prv, B("DG"))
    arrive("xg", prv, R("XG", 0, V)); arrive("bg", prv, R("BG", 0, V))
    for t in range(2):
        arrive("lx%d" % t, prv, B("LX%d" % t)); arrive("lt%d" % t, prv, B("LT%d" % t))
    arrive("lm", nxt, B("LM"))

    if turn_out:
        dma("y", B("NI", 1), T.mp[0:8:2, :])
        dma("s", B("NI", 0, p=S_(0, 32)), T.mp[7:8, :], "ni")
        dma("s", B("NI", 0, p=S_(32, 128)), T.mp[1:7:2, :], "ni")
    else:
        dma("y", B("NI", 1), T.mp[1:8:2, :])
        dma("s", B("NI", 0), T.mp[0:8:2, :])
    dma("y", R("BH", 0, V), T.nb[:])
    bs, xs = ("BS", "XS") if turn_out else ("BH", "XH")
    dma("y", R("XH", 0, V), T.x[:])
    dma("y", B("KN", 0), T.ky[:])
    dma("y", B("KN", 1), T.iv[:])
    if turn_out:
        turn("XS", lambda a, b: T.x[a:b, :], "xs")
        turn("BS", lambda a, b: T.nb[a:b, :], "bs")
    dma("y", R("KI", 0, V), R("XH", 0, V))
    dma("y", R("Mt", 0, V), R("XH", 0, V))

    iota(B("TI"), [[1, 17]], 0, 1, False)
    iota(B("IA"), [[1, 256]], 0, 0)
    iota(B("GM"), [[1, 8], [0, 16]], 0, 0)
    mset(B("ON"), 1.0)
    mset(R("CT", 128, 136), 9999.0)
    ts(B("TJ"), B("TI"), 15, AND)
    ts(col("TG", 0), col("TI", 0), 4, SHR)
    ts(col("TG", 1), col("TI", 0), 4, SHR, 1, AND)
    P, P15, GI, G16, WT, VD, OD, EV, PC, CM, CK, CI_, CV, NG = range(14)
    cf = lambda k: col("CF", k)
    e16 = lambda k: col("E16", k)
    copy(cf(P), col("TI", 0))
    copy(cf(P15), col("TJ", 0))
    copy(cf(GI), col("TG", 0))
    ts(cf(G16), col("TG", 0), 16.0, A.mult)
    ts(cf(WT), col("TG", 0), 16.0, A.mult, 15.0, A.add)
    ts(cf(VD), col("TJ", 0), 2.0, A.mult, 2048.0, A.add)
    ia = lambda k: R("IA", 0, k)
    ts(B("IH"), ia(128), cf(P), A.is_equal)
    ts(B("E16"), ia(16), cf(P15), A.is_equal)
    ts(B("NB"), B("GM"), cf(GI), A.is_equal, -1.0, A.mult)
    ts(B("G8"), ia(8), cf(GI), A.is_equal)
    ts(B("BO"), B("GM"), cf(GI), A.is_equal)
    asel(B("NU"), B("NB"), [[-1, 128]], A.is_gt, 0.0, 0, 1)
    ts(B("W1"), ia(144), cf(WT), A.is_equal)
    for nm in ["BH", "F", "BG"]:
        ts(R(nm, V, V + 32), ia(32), 0.0, A.mult, cf(VD), A.add)
    for nm in ["XH", "XG"]:
        mset(R(nm, V, V + 32), 0.0)
    lin(B("I16"), B("IH"), 16.0)
    for s in range(16):
        lin(B("DS", s), B("IH"), e16(s))
    act(B("ID"), B("IH"), AF.Copy)
    lin(B("IS"), B("IH"), -524288.0)
    lin(B("IP"), B("IH"), 67108864.0)
    lin(B("I3"), B("IH"), 3.0)
    lin(B("G8S"), B("G8"), 32768.0)

    def turns():
        ts(col("TG", 2), col("TI", 0), 112, A.add)
        ts(col("TG", 3), col("TI", 16), 127, AND)
        ts(col("TG", 2), col("TG", 2), 127, AND)
        copy(R("CF", 14, 16), R("TG", 2, 4))
        ts(B("RB"), ia(128), cf(14), A.is_equal)
        ts(B("RF"), ia(128), cf(15), A.is_equal)

    def win(name, i):
        return R(name, 15 - i, 143 - i)

    def search(src, first, btab, wl, after_flags, gap1, gap2):
        ts(B("FL"), src, 2047.5 if first else 0.0, A.is_gt)
        after_flags()
        add("v", lambda: g.vector.tensor_tensor_scan(T.RS[:], T.FL[:], T.FL[:], 0.0, A.add, A.max), [B("FL")], [B("RS")])
        mm(PS(6, 0, 8), B("RS"), B("G8"))
        mm(PS(5, 0, 128), B("BO"), B("RS"), True, False)
        mm(PS(5, 0, 128), B("NU"), B("FL"), False, True)
        copy(B("CB"), PS(6, 0, 8))
        copy(R("CT", 0, 128), PS(5, 0, 128))
        for k in range(8):
            ts(B("C1", ALL, k, ALL), ia(256), col("CB", k), A.is_ge)
        for c in range(16):
            mm(PS(4, c, c + 1), B("C1", c), col("ON", 0))
        gap1()
        copy(B("BL"), PS(4, 0, 16))
        copy(B("BB"), PS(4, 0, 16))
        tt(B("C2"), IND(B("CT"), B("BL")), ia(256), A.is_le)
        mm(PS(3, 0, 16), B("I16"), B("BB"), True, False)
        for i in range(16):
            mm(PS(3, 0, 16), win("W1", i), R("C2", i, 256, 16), False, i == 15)
        gap2()
        copy(R(wl, 256, 272), PS(3, 0, 16))
        if first and turn_out:
            copy(B("UH"), PS(3, 0, 16))
            mm(PS(4, 0, 16), B("RB"), B("UH"))
            copy(B("UN"), PS(4, 0, 16))
            copy(R("WH", 0, 256), IND(B(btab), B("UN")))
            mm(PS(5, 0, 256), B("RF"), R("WH", 0, 256))
            copy(R("WH", 256, 512), IND(R("XH", 0, 2064), B("UN")))
            mm(PS(6, 0, 256), B("RF"), R("WH", 256, 512))
            copy(R(wl, 0, 256), PS(5, 0, 256))
        else:
            copy(R(wl, 0, 256), IND(B(btab), R(wl, 256, 272)))

    def number_rows(b, stop):
        mm(PS(b, 0, 256), B("DS", 12), B("UB"), True, False)
        mm(PS(b, 0, 256), win("W1", 13), B("C2"), False, stop)

    for k in range(2):
        copy(B("NF", ALL, k, ALL), B("NI", k))
    for e in range(4):
        add("v", lambda e=e: g.vector.transpose(T.MW[:, e:128:4], T.NF[:, e]), [B("NF", e)], [R("MW", e, 128, 4)])

    def first_list():
        copy(B("sML"), B("MW"))
        send("ml", nxt, ("ML", 0, 128), B("sML"))
        iota(B("QR", ALL, 7), [[128, 2], [0, 8]], 0, 1)
        iota(B("QL", ALL, 11), [[128, 2], [0, 8]], 0, 1)
        iota(B("T3"), [[16, 16]], 0, 1)
        for o, k, c in [(B("QR", ALL, 10), 16, 256), (B("QR", ALL, 11), 16, 1), (B("QR", ALL, S_(12, 16)), 64, 0),
                        (B("QL", ALL, 4), 16, -256), (B("QL", ALL, S_(5, 7)), 32, -int(BIG)), (B("QL", ALL, 7), 16, -1),
                        (B("QL", ALL, S_(12, 16)), 64, 0), (B("CQ", ALL, 4), 16, 16), (B("H4"), 4, 8192)]:
            iota(o, [[0, k]], c, 0)

    def digits_m():
        ni = B("NI")
        if turn_out:
            turns()
        ts(B("DI", 0), ni, 7, AND)
        ts(B("DI", 1), ni, 3, SHR, 7, AND)
        ts(B("DI", 2), ni, 6, SHR, 7, AND)
        ts(B("DI", 3), ni, 9, SHR)
        lin(cf(CM), e16(1), 8.0, e16(0))
        lin(cf(OD), col("TG", 1), 1.0)
        lin(cf(EV), col("TG", 1), -1.0, 1.0)
        lin(cf(CM), e16(2), 64.0, cf(CM))
        lin(cf(PC), cf(P15), 8.0, cf(GI))
        lin(cf(CK), e16(14), 32.0, e16(4))
        lin(cf(CM), e16(3), 512.0, cf(CM))
        lin(cf(CI_), e16(12), 16.0, e16(13))
        lin(cf(CV), e16(3), 4.0, -3.5)
        lin(cf(NG), cf(G16), -1.0)
        lin(B("JC"), B("TJ"), 1.0 / 32768)
        lin(B("sDG"), B("DI"), 1.0, -3.5)

    search(B("MW"), True, "BH", "sWL", first_list, digits_m, lambda: copy(B("UB"), IND(B("IA"), B("BL"))))
    send("wl", nxt, ("WL", 0, 272), B("sWL"))
    number_rows(2, True)
    copy(R("sXU", 0, 256), PS(6, 0, 256) if turn_out else IND(R("XH", 0, 2064), R("sWL", 256, 272)))
    copy(R("sXU", 256, 512), PS(2, 0, 256))
    send("xu", nxt, ("XU", 0, 512), B("sXU"))
    send("dg", nxt, ("DG", 0, 4), B("sDG"))
    if not turn_out:
        send("xg", nxt, ("XG", 0, V), R(xs, 0, V))
        send("bg", nxt, ("BG", 0, V), R(bs, 0, V))

    def gather_f():
        act(R("F", 0, V), IND(B("BH"), B("ML")), AF.Copy)

    gather_f()
    lin(R("DU", 0, 16), B("T3"), 1.0, cf(NG))
    for nm, c in [("WM", CM), ("WK", CK), ("WI", CI_), ("WB", CK)]:
        lin(B(nm), B("W1"), cf(c))
    lin(R("DU", 16, 32), R("DU", 0, 16), 1.0, 2048.0)
    lin(R("DU", 32, 48), R("DU", 0, 16), 2.0, 2304.0)
    lin(R("MV", 256, 512), ia(256), 0.0, cf(CV))
    lin(B("CQ", ALL, S_(0, 4)), ia(64), 0.0, 3.5)
    lin(B("QR", ALL, S_(8, 10)), ia(32), 0.0, -0.5)
    ts(B("TC"), R("TJ", 0, 16), cf(G16), A.add)
    for k in range(1, 9):
        ts(B("DM", k - 1), ia(128), col("TC", 16 - k), A.is_equal)
    asel(B("DM"), B("DM"), [[0, 8], [-1, 128]], A.not_equal, -1.0, 0, 1)
    if turn_out:
        send("xg", nxt, ("XG", 0, V), R(xs, 0, V))
    ts(B("DI2", 2), B("KN", 1), 4, SHR)
    ts(B("NO"), B("KN", 1), 2047.5, A.is_gt, 122.0, A.mult)
    ts(B("DI2", 0), B("KN", 0), 31, AND)
    ts(B("DI2", 1), B("KN", 0), 5, SHR)
    ts(B("DI2", 3), B("KN", 1), 15, AND)
    tt(B("DI2", 2), B("DI2", 2), B("NO"), A.add)
    for k in range(4):
        for c in range(2):
            dma("y", B("Mt", S_(0, V), p=S_(16 * c + k, 128, 32)), B("DG", k, c), "mt")

    def late_constants():
        for k in range(1, 8):
            ts(B("ZM", k - 1), ia(128), col("TC", k), A.is_equal)
        asel(B("ZM"), B("ZM"), [[0, 7], [-1, 128]], A.not_equal, 1.0, 0, 1)
        if turn_out:
            send("bg", nxt, ("BG", 0, V), R(bs, 0, V))
        ts(B("PM"), ia(128), cf(PC), A.is_equal)

    for t in range(3):
        last = t == 2
        mine = (0, 1, 4)

        def rg(c):
            o, i = R("R16", 512 * c, 512 * c + 512), IND(B("F"), R("WL", 32 * c, 32 * c + 32))
            if c in mine:
                copy(o, i)
            else:
                act(o, i, AF.Copy)

        def pick(qr):
            b = 6 if qr < 2 else 1
            for s in range(16):
                j = (s - t) % 16
                mm(PS(b, 64 * (qr % 2), 64 * (qr % 2) + 64), B("DS", s), R("R16", 1024 * qr + j, 1024 * qr + 1024, 16), s == 0, s == 15)
        if t > 0:
            copy(R("XU", 0, 256), IND(R("XG", 0, 2064), R("WL", 256, 272)))
        own = 6 if t == 0 else 0
        if t == 0:
            for c in (0, 2, 1, 3):
                rg(c)
            late_constants()
        for s in range(own, 16):
            asel(R("XR", 2048 + s, 4096, 16), R("XU", 128, 256), [[0, 128]], A.is_gt, 0.0, 1, 0)
        for c in (4, 5, 6, 7) if t == 0 else (0, 2, 1, 3, 4, 5, 6, 7):
            rg(c)
        for qr in range(4):
            pick(qr)
        for s in range(16):
            w = 256 if s < own else 128
            copy(R("XR", s, 16 * w, 16), R("XU", 0, w))
        copy(R("VL", 0, 128), PS(6, 0, 128))
        if t == 0:
            act(B("DK"), B("DI2"), AF.Copy)
            for k, row in enumerate([4, 14, 12, 13]):
                dma("y", B("KI", S_(0, V), p=S_(row, 128, 16)), B("DK", k), "ki")
        act(R("VH", 0, 128), PS(6, 0, 128), AF.Copy)
        act(R("VH", 128, 256), PS(1, 0, 128), AF.Copy)
        for k in range(8):
            mm(PS(2 + k // 2, 256 * (k % 2), 256 * (k % 2) + 256), B("DM", k), B("VH"))
        cb = [0, 7]
        for h in range(2):
            mm(PS(cb[h], 0, 128), R("VH", 128 * h, 128 * h + 128), B("IH"), True, False)

        def xg(lo, hi):
            tt(R("E", 16 * lo, 16 * hi), IND(R("XH", 0, 2080), R("VL", lo, hi)), R("XR", 16 * lo, 16 * hi), A.subtract)

        def ab(lo, hi):
            act(R("E", 16 * lo, 16 * hi), R("E", 16 * lo, 16 * hi), AF.Abs)

        def dsum(h, stop):
            for s in range(16):
                mm(PS(cb[h], s, 128, 16), R("E", 2048 * h + s, 2048 * h + 2048, 16), B("G8S"), False, stop and s == 15)

        def cterm(h, stop):
            mm(PS(cb[h], 0, 128), R("S1", 128 * h, 128 * h + 128), B("IS"), False, False)
            mm(PS(cb[h], 0, 128), R("S2", 128 * h, 128 * h + 128), B("IP"), False, stop)

        def best(h, between=()):
            for k in range(8):
                o, i = col("CI", 8 * h + k), PS(cb[h], 16 * k, 16 * k + 16)
                add("v", lambda o=o, i=i: g.vector.tensor_reduce(o[0], i[0], AX.X, A.min), [i], [o])
                if k < len(between):
                    between[k]()
        xg(0, 64)
        copy(R("VL", 128, 256), PS(1, 0, 128))
        xg(64, 128)
        for k in range(4):
            act(R("AD", 512 * k, 512 * k + 512), PS(2 + k, 0, 512), AF.Abs)
        for k in range(2):
            ts(R("EQ", 1024 * k, 1024 * k + 1024), R("AD", 1024 * k, 1024 * k + 1024), 0.5, A.is_lt)
        for k in range(8):
            mm(PS(6, 0, 256), B("ZM", k) if k < 7 else B("ID"), R("EQ", 256 * k, 256 * k + 256), k == 0, k == 7)
        ab(0, 64)
        xg(128, 192)
        act(B("S1"), PS(6, 0, 256), AF.Copy)
        ab(64, 128)
        ts(B("S2"), B("S1"), 0.5, A.is_lt, col("JC", (16 - t) % 16), A.add)
        xg(192, 232)
        copy(B("UF"), R("WL", 256, 272))
        xg(232, 256)
        cterm(0, False)
        dsum(0, True)
        cterm(1, False)
        ab(128, 192)
        ab(192, 232)
        ab(232, 256)
        best(0, [lambda: ts(B("U2"), B("UF"), 2047.5, A.is_gt), lambda: tt(B("U4"), B("U2"), R("DU", 0, 16), A.mult),
                 lambda: tt(B("U2"), B("U4"), B("UF"), A.add), lambda: copy(B("SU"), B("U2")), lambda: ts(B("U4"), B("U2"), 4096.0, A.add)])
        if t > 0:
            act(B("UB"), IND(B("IA"), B("BL")), AF.Copy)
        dsum(1, True)
        if t == 0:
            mm(PS(1, 0, 256), B("ID"), R("XU", 256, 512), True, False)
        else:
            number_rows(1, False)
        best(1)
        ts(B("QI", ALL, 0), B("CI"), 7, AND)
        ts(B("QI", ALL, 1), B("CI"), 3, SHR, 7, AND)
        ts(B("QI", ALL, 2), B("CI"), 6, SHR, 7, AND)
        ts(B("QI", ALL, 3), B("CI"), 9, SHR, 3, AND)
        ts(B("QI", ALL, 4), B("CI"), 15, SHR)
        dg = B("QI", ALL, S_(0, 4))
        act(B("SQ"), dg, AF.Square, bias=-3.5)
        act(B("SL"), dg, AF.Square, bias=-1792.0, scale=512.0)
        ts(B("QL", ALL, S_(0, 4)), dg, -3.5, A.add, 2 * BIG, A.mult)
        tt(B("QR", ALL, S_(0, 5)), B("QI"), B("CQ"), A.subtract)
        ts(B("QL", ALL, 10), B("QI", ALL, 4), -16.0, A.add)
        tt(B("QR", ALL, S_(5, 7)), B("SQ", ALL, S_(0, 2)), B("SQ", ALL, S_(2, 4)), A.add)
        tt(B("QL", ALL, S_(8, 10)), B("SL", ALL, S_(0, 2)), B("SL", ALL, S_(2, 4)), A.add)
        for h in range(2):
            mm(PS(1, 128 * h, 128 * h + 128), B("QR", S_(8 * h, 8 * h + 8)), B("ID"), False, h == 1)
        for h in range(2):
            mm(PS(2, 128 * h, 128 * h + 128), B("QL", S_(8 * h, 8 * h + 8)), B("PM"))
        zr = R("MV", 0, 256)
        copy(zr, PS(1, 0, 256))
        lin(B("ZE"), PS(2, 0, 256), cf(EV))
        lin(B("ZO"), PS(2, 0, 256), cf(OD))

        def wrap(lo, w, src):
            for i in range(16):
                mm(PS(6, lo, lo + 16), win(w, i), R(src, i, 256, 16), i == 0, i == 15)
        wrap(0, "WM", "MV")
        copy(IND(B("Mt"), B("SU")), zr)
        ub = [4, 5, 0, 7, 3, 2, 4, 5]

        def form(u):
            H, pp = u // 4, S_(32 * (u % 4), 32 * (u % 4) + 32)
            for k in range(4):
                mm(PS(ub[u], 128 * k, 128 * k + 128), B("MV", S_(128 * (k // 2), 128 * (k // 2) + 128), p=pp),
                   B("ZO" if k % 2 else "ZE", S_(128 * H, 128 * H + 128), p=pp))

        def beaten(u):
            o = B("LO", u // 4, S_(2 * (u % 4), 2 * (u % 4) + 2))
            act(o, PS(ub[u], 0, 256), AF.Relu)
            tt(o, PS(ub[u], 256, 512), o, A.max)

        def count(H):
            for c in range(8):
                mm(PS(1, 256 + 8 * H + c, 288, 16), B("LO", H, ALL, S_(c, 128, 8)), R("H4", 0, 2), False, H == 1 and c == 7)
        for u in range(6):
            form(u)
        ts(B("VW"), PS(6, 0, 16), 2047.5, A.add)
        ts(R("XB", 16, 32), PS(6, 0, 16), 2047.5, A.add)
        tt(B("KS"), IND(R("KI", 0, V), B("VW")), zr, A.subtract)
        beaten(0)
        beaten(1)
        form(6)
        form(7)
        beaten(2)
        beaten(3)
        wrap(16, "WI", "KS")
        wrap(32, "WK", "KS")
        for u in range(4, 8):
            beaten(u)
        if not last:
            act(B("T1"), IND(R("XH", 0, V), B("VW")), AF.Copy)
            mm(PS(2, 0, 256), B("I3"), B("T1"), True, False)
            mm(PS(2, 0, 256), B("ID"), R("XU", 0, 256), False, True)
            lin(B("T2"), PS(2, 0, 256), 0.25, 191.625)
            lin(B("XN"), B("T2"), 1.0, -192.0)
            send("lx%d" % t, nxt, ("LX%d" % t, 0, 256), B("XN"))
        tt(B("O1"), PS(6, 16, 32), B("UF"), A.add)
        ts(B("PN"), PS(6, 32, 48), 0.5, A.is_lt, 8192.0, A.mult)
        tt(R("XB", 0, 16), B("O1"), R("DU", 32, 48), A.min)
        mm(PS(1, 256, 288), B("IH"), B("XB"), True, False)
        for k in range(2):
            mm(PS(1, 256 + 16 * k, 272 + 16 * k), B("IH"), B("PN"), False, False)
        count(0)
        count(1)
        tt(B("TA"), PS(1, 256, 272), B("U4"), A.min)
        tt(B("T3"), PS(1, 272, 288), R("DU", 16, 32), A.min)
        ts(B("TB"), B("TA"), 4095, AND)
        tv = B("TV")
        copy(tv, B("T3"))
        copy(B("TL"), B("TB"))
        if not last:
            send("lt%d" % t, nxt, ("LT%d" % t, 0, 16), tv)
        copy(IND(B("Mt"), B("TL")), R("MV", 256, 512))
        if last:
            for i in range(16):
                mm(PS(0, 0, 128), win("WM", i), R("Mt", 128 * i, 128 * i + 128), i == 0, i == 15)
            copy(IND(B("KI"), tv), zr)
            lin(B("MO"), PS(0, 0, 128), 1.0, 2047.5)
            send("lm", prv, ("LM", 0, 128), B("MO"))
            for i in range(16):
                mm(PS(2, 0, 128), win("WB", i), R("KI", 128 * i, 128 * i + 128), i == 0, i == 15)
            copy(B("KO"), PS(2, 0, 128))
            dma("y", T.yk[:], B("KO"))
            if turn_out:
                dma("s", T.ym[0:7, :], B("LM", p=S_(16, 128)))
                dma("y", T.ym[7:8, :], B("LM", p=S_(0, 16)))
            else:
                dma("s", T.ym[:], B("LM"))
        else:
            for i in range(16):
                mm(PS(0, 0, 128), win("WM", i), R("Mt", i, V, 16), i == 0, i == 15)
            copy(IND(B("KI"), tv), zr)
            lx, lt = "LX%d" % t, "LT%d" % t
            if turn_in:
                turn("RX", lambda a, b: B(lx, p=S_(a, b)), "rx%d" % t)
                turn("RT", lambda a, b: B(lt, p=S_(a, b)), "rt%d" % t)
                lx, lt = "RX", "RT"

            def next_list():
                ts(B("ML"), PS(0, 0, 128), 2047.5, A.add)
                gather_f()
            search(PS(0, 0, 128), False, "BG", "WL", next_list, lambda: copy(IND(B("XH"), tv), B("XN")),
                   lambda: copy(IND(B("XG"), B(lt)), B(lx)))

    pos = {}
    cnt = {k: 0 for k in COMPUTE}
    for i, o in enumerate(ops):
        if o["sem"] is None:
            cnt[o["q"]] += 1
            pos[i] = cnt[o["q"]]
    known = {k: {} for k in Q}
    need = set()
    for i, o in enumerate(ops):
        if o["q"] is None:
            o["seen"] = {}
            continue
        kn = known[o["q"]]
        o["waits"] = []
        for d in sorted(o["deps"], reverse=True):
            key, val = (ops[d]["q"], pos[d]) if ops[d]["sem"] is None else (ops[d]["sem"][0], 1)
            if kn.get(key, 0) >= val:
                continue
            o["waits"].append(d)
            need.add(d)
            kn[key] = val
            for k2, v2 in ops[d]["seen"].items():
                if kn.get(k2, 0) < v2:
                    kn[k2] = v2
        o["seen"] = dict(kn)
    val = {}
    cnt = {k: 0 for k in COMPUTE}
    for i, o in enumerate(ops):
        if o["sem"] is None and i in need:
            cnt[o["q"]] += 1
            val[i] = cnt[o["q"]]
    for i, o in enumerate(ops):
        if o["q"] is None:
            continue
        for d in o["waits"]:
            if ops[d]["sem"] is None:
                Q[o["q"]].wait_ge(T.sem[COMPUTE[ops[d]["q"]]], val[d])
            else:
                Q[o["q"]].wait_ge(T.sem[ops[d]["sem"][0]], ops[d]["sem"][1])
        ins = o["fn"]()
        if o["sem"] is None:
            if i in need:
                ins.then_inc(T.sem[COMPUTE[o["q"]]], 1)
        elif o["sem"][0][0] == "d":
            ins.then_inc(T.sem[o["sem"][0]], 16)
    for i, o in enumerate(ops):
        if o["sem"] is not None and i not in need:
            g.wait_ge(T.sem[o["sem"][0]], o["sem"][1])
